import numpy as np
import ml_dtypes


def mxq(x, axis, fmt="e4m3"):
    dtype, down = {"e4m3": (ml_dtypes.float8_e4m3fn, 7), "e5m2": (ml_dtypes.float8_e5m2, 14)}[fmt]
    v = np.moveaxis(np.asarray(x, np.float32).astype(ml_dtypes.bfloat16).astype(np.float64), axis, -1)
    blocks = v.reshape(v.shape[:-1] + (-1, 32))
    amax = np.abs(blocks).max(-1, keepdims=True)
    byte = np.maximum(np.where(amax > 0, np.frexp(amax)[1] - 1 + 127, 0) - down, 1)
    scale = np.exp2(byte - 127.0)
    codes = (blocks / scale).astype(np.float32).astype(dtype).astype(np.float64)
    return np.moveaxis((codes * scale).reshape(v.shape), -1, axis)


WIDE = False


def mx_kscale(k):
    if not WIDE:
        return np.ones(k)
    levels = np.array([10, -10, 5, -5, 0])
    if k % 512:
        return np.exp2(np.random.permutation(np.resize(levels, k // 32))).repeat(32)
    a = np.empty((k // 512, 16))
    for p in range(k // 512):
        a[p, :8] = np.random.permutation(np.resize(levels, 8))
        for g in range(8):
            far = levels[np.abs(levels - a[p, g]) >= 10]
            a[p, g + 8] = far[np.random.randint(len(far))]
    return np.exp2(a.ravel()).repeat(32)


def f64(x):
    return np.asarray(x).astype(np.float64)


def striped(idx):
    return np.tile(idx.reshape(-1, 16).T, (8, 1)).astype(np.uint16)


def unstriped(offs):
    return offs[:16].T.reshape(-1).astype(np.int64)


def striped8(idx):
    return np.concatenate([x.reshape(-1, 16).T for x in idx]).astype(np.uint16)


def runs(offs, k):
    lists = np.stack([offs[16 * r : 16 * r + 16].T.reshape(-1) for r in range(8)]).astype(np.int64)
    return lists[np.arange(k) % 512 // 64]


def pack_weight(w):
    k, n = w.shape
    w = f64(np.asarray(w, np.float32).astype(ml_dtypes.bfloat16)).reshape(k // 32, 32, n)
    amax = np.abs(w).max(1)
    byte = np.clip(np.where(amax > 0, np.frexp(amax)[1] - 1 + 127 - 7, 1), 1, 254)
    scaled = (w * np.exp2(127.0 - byte)[:, None, :]).reshape(k, n).astype(np.float32)
    words = np.ascontiguousarray(scaled.reshape(k // 512, 128, 4, n).transpose(0, 1, 3, 2)).astype(ml_dtypes.float8_e4m3fn).view(np.uint8)
    return words, np.ascontiguousarray(byte.astype(np.uint8).reshape(k // 512, 16, n))


def unpack_weight(words, scales):
    g, p, n, _ = words.shape
    vals = np.ascontiguousarray(words).view(ml_dtypes.float8_e4m3fn).astype(np.float64) * np.repeat(np.exp2(scales.astype(np.float64) - 127.0), 8, axis=1)[..., None]
    return vals.transpose(0, 1, 3, 2).reshape(g * 512, n)


K, T, S, N, H = 512, 2048, 512, 512, 512


def setup_inputs():
    n = np.random.standard_normal
    s = mx_kscale(K)[:, None]
    u = mx_kscale(H)
    packed_xT = pack_weight(n((K, T)) * s)
    return {
        "x_words": packed_xT[0],
        "x_scales": packed_xT[1],
        "w1": (n((K, H)) / np.sqrt(K) / s).astype(np.float32),
        "w2": (n((K, H)) / np.sqrt(K) / s).astype(np.float32),
        "gn": (np.random.uniform(0.5, 1.5, (H, 1)) * u[:, None]).astype(np.float32),
        "w3": (n((H, N)) / np.sqrt(H) / u[:, None]).astype(np.float32),
        "offs": striped(np.random.permutation(T)[:S]),
        "two": striped(np.random.permutation(T)[:S]),
        "p1": striped8(np.stack([np.random.permutation(S) for _ in range(8)])),
        "p2": striped8(np.stack([np.random.permutation(S) for _ in range(8)])),
    }


def reference(x_words, x_scales, w1, w2, gn, w3, offs, two, p1, p2):
    xq = unpack_weight(x_words, x_scales)[:, unstriped(offs)]
    y = mxq(f64(w1), 0, "e4m3").T @ xq
    k1 = np.exp(-0.5 * ((y - (y[np.arange(H)[:, None], runs(p1, H)])) ** 2))
    x_two = unpack_weight(x_words, x_scales)[:, unstriped(two)]
    c = mxq(f64(w2), 0, "e4m3").T @ x_two
    k2 = np.exp(-0.5 * ((y - (y[np.arange(H)[:, None], runs(p2, H)])) ** 2))
    z = f64(gn) * ((k1 * (c[np.arange(H)[:, None], runs(p1, H)]) + k2 * (c[np.arange(H)[:, None], runs(p2, H)])) / (k1 + k2 + 0.5))
    return mxq(f64(w3), 0, "e4m3").T @ mxq(z, 0, "e4m3")

@@ -1,0 +1,203 @@
+from contextlib import ExitStack
+
+import concourse.mybir as mybir
+from concourse.masks import make_identity
+
+K, T, S, N, H = 512, 2048, 512, 512, 512
+FLOPS = 2 * K * H * S * 2 + 2 * H * N * S
+
+F32 = mybir.dt.float32
+BF16 = mybir.dt.bfloat16
+I32 = mybir.dt.int32
+U32 = mybir.dt.uint32
+U16 = mybir.dt.uint16
+U8 = mybir.dt.uint8
+FP8X4 = mybir.dt.float8_e4m3fn_x4
+ALU = mybir.AluOpType
+ACT = mybir.ActivationFunctionType
+
+P = 128
+PACK = 4
+HALF = S // 2
+
+
+def tile_picked_kerndens_none_p_kernel(
+    tc, x_words, x_scales, w1, w2, gn, w3, offs, two, p1, p2, out
+):
+    nc = tc.nc
+    with ExitStack() as ctx:
+        keep = ctx.enter_context(tc.tile_pool(name="keep", bufs=1))
+        psum = ctx.enter_context(tc.psum_pool(name="psum", bufs=1))
+
+        def bank(b):
+            return psum.tile([P, 512], F32, name="bank%d" % b)
+
+        def sb(name, shape, dtype):
+            return keep.tile(shape, dtype, name=name, align_bytes=64)
+
+        offs_sb = keep.tile([P, S // 16], U16, name="offs_sb")
+        two_sb = keep.tile([P, S // 16], U16, name="two_sb")
+        p1_sb = keep.tile([P, S // 16], U16, name="p1_sb")
+        p2_sb = keep.tile([P, S // 16], U16, name="p2_sb")
+        xs_sb = sb("xs_sb", [P, T], U8)
+        xw_sb = sb("xw_sb", [P, T], I32)
+        nc.sync.dma_start(offs_sb[:], offs)
+        nc.sync.dma_start(two_sb[:], two)
+        for q in range(4):
+            rows = x_scales[0, 4 * q : 4 * q + 4, :].bitcast(I32)
+            nc.sync.dma_start(
+                xs_sb[32 * q : 32 * q + 32, :].bitcast(I32), rows.unsqueeze(0).broadcast_to([8, 4, T // 4])
+            )
+        nc.sync.dma_start(xw_sb[:], x_words[0].rearrange("p n t -> p (n t)").bitcast(I32))
+        w1_raw = []
+        for h in range(2):
+            raw = sb("w1_raw%d" % h, [P, PACK, H // 2], F32)
+            nc.sync.dma_start(raw[:], w1[:, h * 256 : (h + 1) * 256].rearrange("(p j) c -> p j c", j=PACK))
+            w1_raw.append(raw)
+        nc.sync.dma_start(p1_sb[:], p1)
+        nc.sync.dma_start(p2_sb[:], p2)
+        w2_raw = sb("w2_raw", [P, PACK, H], F32)
+        nc.sync.dma_start(w2_raw[:], w2.rearrange("(p j) c -> p j c", j=PACK))
+        gn_sb = sb("gn_sb", [P, PACK], F32)
+        nc.sync.dma_start(gn_sb[:], gn.rearrange("(p t) o -> p (t o)", t=PACK))
+        w3_raw = sb("w3_raw", [P, PACK, N], F32)
+        nc.sync.dma_start(w3_raw[:], w3.rearrange("(p j) c -> p j c", j=PACK))
+
+        ident = sb("ident", [P, P], F32)
+        make_identity(nc, ident[:])
+        y_win = [sb("y_win%d" % t, [P, 2 * S], F32) for t in range(PACK)]
+        for t in range(PACK):
+            nc.gpsimd.memset(y_win[t][:, S:], 0.0)
+
+        xa_s = sb("xa_s", [P, S], U8)
+        xb_s = sb("xb_s", [P, S], U8)
+        xa_w = sb("xa_w", [P, S], U32)
+        xb_w = sb("xb_w", [P, S], U32)
+        nc.vector.tensor_copy(xa_s[:], xs_sb[:].indirect(offs_sb[:]))
+        nc.vector.tensor_copy(xb_s[:], xs_sb[:].indirect(two_sb[:]))
+        nc.vector.tensor_copy(xa_w[:], xw_sb[:].bitcast(U32).indirect(offs_sb[:]))
+        nc.vector.tensor_copy(xb_w[:], xw_sb[:].bitcast(U32).indirect(two_sb[:]))
+
+        w1_g = sb("w1_g", [P, PACK * H], BF16)
+        w1_gv = w1_g[:].rearrange("p (t m j) -> p m j t", t=PACK, j=PACK)
+        nc.scalar.copy(w1_gv[:, 0:64], w1_raw[0][:].rearrange("p j (m t) -> p m j t", t=PACK))
+        nc.vector.tensor_copy(w1_gv[:, 64:128], w1_raw[1][:].rearrange("p j (m t) -> p m j t", t=PACK))
+        w1_c = sb("w1_c", [P, H], U32)
+        w1_s = sb("w1_s", [P, H], U8)
+        y_cp = [sb("y_cp%d" % t, [P, S], F32) for t in range(PACK)]
+        for t in range(PACK):
+            cols = slice(t * P, (t + 1) * P)
+            nc.vector.quantize_mx(out=w1_c[:, cols].bitcast(FP8X4), scales=w1_s[:, cols], in_=w1_g[:, t * 512 : (t + 1) * 512])
+            acc = bank(t)
+            nc.tensor.matmul_mx(
+                out=acc[:], lhsT=w1_c[:, cols].bitcast(FP8X4), lhsT_scale=w1_s[:, cols],
+                rhs=xa_w[:].bitcast(FP8X4), rhs_scale=xa_s[:], start=True, stop=True,
+            )
+            nc.scalar.copy(y_win[t][:, :S], acc[:])
+            if t == 0:
+                nc.vector.tensor_copy(y_cp[t][:], y_win[t][:, :S])
+            else:
+                nc.sync.dma_start(y_cp[t][:], y_win[t][:, :S])
+
+        w2_g = sb("w2_g", [P, PACK * H], BF16)
+        nc.vector.tensor_copy(
+            w2_g[:].rearrange("p (t m j) -> p m j t", t=PACK, j=PACK), w2_raw[:].rearrange("p j (m t) -> p m j t", t=PACK)
+        )
+        w2_c = sb("w2_c", [P, H], U32)
+        w2_s = sb("w2_s", [P, H], U8)
+        nc.vector.quantize_mx(out=w2_c[:].bitcast(FP8X4), scales=w2_s[:], in_=w2_g[:])
+
+        kk = []
+        c_win = []
+        for t in range(PACK):
+            d = sb("d%d" % t, [P, 2 * S], F32)
+            nc.vector.tensor_tensor(d[:, :S], y_win[t][:].indirect(p1_sb[:]), y_cp[t][:], ALU.subtract)
+            nc.vector.tensor_tensor(d[:, S:], y_win[t][:].indirect(p2_sb[:]), y_cp[t][:], ALU.subtract)
+            sq = sb("sq%d" % t, [P, 2 * S], F32)
+            nc.scalar.activation(sq[:], d[:], ACT.Square)
+            k = sb("k%d" % t, [P, 2 * S], F32)
+            nc.scalar.activation(k[:], sq[:], ACT.Exp, scale=-0.5)
+            kk.append(k)
+            cols = slice(t * P, (t + 1) * P)
+            acc = bank(4 + t)
+            nc.tensor.matmul_mx(
+                out=acc[:], lhsT=w2_c[:, cols].bitcast(FP8X4), lhsT_scale=w2_s[:, cols],
+                rhs=xb_w[:].bitcast(FP8X4), rhs_scale=xb_s[:], start=True, stop=True,
+            )
+            cw = sb("c_win%d" % t, [P, S], F32)
+            nc.scalar.activation(cw[:], acc[:], ACT.Copy, scale=gn_sb[:, t : t + 1])
+            c_win.append(cw)
+
+        den = [bank(b) for b in range(4)]
+        for t in range(PACK):
+            for b in range(4):
+                for s in range(2):
+                    nc.tensor.matmul(
+                        den[b][:, t * P : (t + 1) * P], lhsT=kk[t][:, s * S + b * P : s * S + (b + 1) * P], rhs=ident[:],
+                        is_transpose=True, start=(s == 0), stop=(s == 1),
+                    )
+        rr = []
+        for b in range(4):
+            dsq = sb("dsq%d" % b, [P, H], F32)
+            nc.scalar.activation(
+                dsq[:].rearrange("j (p t) -> j p t", t=PACK), den[b][:].rearrange("j (t p) -> j p t", t=PACK), ACT.Square, bias=0.5
+            )
+            r = sb("r%d" % b, [P, H], F32)
+            nc.scalar.activation(r[:], dsq[:], ACT.Abs_reciprocal_sqrt)
+            rr.append(r)
+
+        w3_g = sb("w3_g", [P, PACK * N], BF16)
+        nc.scalar.copy(
+            w3_g[:].rearrange("p (c i j) -> p c j i", i=4, j=PACK), w3_raw[:].rearrange("p j (c i) -> p c j i", i=4)
+        )
+        w3_c = sb("w3_c", [P, N], U32)
+        w3_s = sb("w3_s", [P, N], U8)
+        nc.vector.quantize_mx(out=w3_c[:].bitcast(FP8X4), scales=w3_s[:], in_=w3_g[:])
+
+        for h in range(2):
+            js = slice(h * HALF, (h + 1) * HALF)
+            ls = slice(h * HALF // 16, (h + 1) * HALF // 16)
+            num = [bank(4 + 2 * h + b) for b in range(2)]
+            for t in range(PACK):
+                n = sb("n%d_%d" % (h, t), [P, 2 * HALF], F32)
+                nc.vector.tensor_tensor(n[:, :HALF], c_win[t][:].indirect(p1_sb[:, ls]), kk[t][:, h * HALF : (h + 1) * HALF], ALU.mult)
+                nc.vector.tensor_tensor(n[:, HALF:], c_win[t][:].indirect(p2_sb[:, ls]), kk[t][:, S + h * HALF : S + (h + 1) * HALF], ALU.mult)
+                for b in range(2):
+                    for s in range(2):
+                        nc.tensor.matmul(
+                            num[b][:, t * P : (t + 1) * P], lhsT=n[:, s * HALF + b * P : s * HALF + (b + 1) * P], rhs=ident[:],
+                            is_transpose=True, start=(s == 0), stop=(s == 1),
+                        )
+            zw = bank(h)
+            for b in range(2):
+                zt = sb("zt%d_%d" % (h, b), [P, H], BF16)
+                nc.vector.tensor_tensor(
+                    zt[:].rearrange("j (p t) -> j p t", t=PACK), num[b][:].rearrange("j (t p) -> j p t", t=PACK),
+                    rr[2 * h + b][:].rearrange("j (p t) -> j p t", t=PACK), ALU.mult,
+                )
+                words = zt[:].bitcast(F32)
+                for u in range(2):
+                    nc.tensor.transpose(zw[:, (2 * b + u) * P : (2 * b + u + 1) * P], words[:, u : H // 2 : 2], ident[:])
+            z_g = sb("z_g%d" % h, [P, PACK * HALF], BF16)
+            nc.scalar.copy(
+                z_g[:].bitcast(F32).rearrange("p (b j u) -> p b j u", b=2, u=2), zw[:].rearrange("p (b u j) -> p b j u", b=2, u=2)
+            )
+            z_c = sb("z_c%d" % h, [P, HALF], U32)
+            z_s = sb("z_s%d" % h, [P, HALF], U8)
+            nc.vector.quantize_mx(out=z_c[:].bitcast(FP8X4), scales=z_s[:], in_=z_g[:])
+            for g in range(2):
+                acc = bank(2 + 2 * h + g)
+                for a in range(2):
+                    cols = slice((2 * g + a) * P, (2 * g + a + 1) * P)
+                    nc.tensor.matmul_mx(
+                        out=acc[:, a * HALF : (a + 1) * HALF], lhsT=w3_c[:, cols].bitcast(FP8X4), lhsT_scale=w3_s[:, cols],
+                        rhs=z_c[:].bitcast(FP8X4), rhs_scale=z_s[:], start=True, stop=True,
+                    )
+                res = sb("res%d_%d" % (h, g), [P, 2 * HALF], F32)
+                if g == 0:
+                    nc.scalar.copy(res[:], acc[:])
+                else:
+                    nc.vector.tensor_copy(res[:], acc[:])
+                nc.sync.dma_start(
+                    out[g * 256 : (g + 1) * 256, js].rearrange("(a p) j -> p a j", a=2), res[:].rearrange("p (a j) -> p a j", a=2)
+                )

@@ -32,8 +32,8 @@ def tile_picked_kerndens_none_p_kernel(
         def bank(b):
             return psum.tile([P, 512], F32, name="bank%d" % b)
 
-        def sb(name, shape, dtype):
-            return keep.tile(shape, dtype, name=name, align_bytes=64)
+        def sb(name, shape, dtype, tag=None):
+            return keep.tile(shape, dtype, name=name, tag=tag or name, align_bytes=64)
 
         offs_sb = keep.tile([P, S // 16], U16, name="offs_sb")
         two_sb = keep.tile([P, S // 16], U16, name="two_sb")
@@ -56,8 +56,11 @@ def tile_picked_kerndens_none_p_kernel(
             w1_raw.append(raw)
         nc.sync.dma_start(p1_sb[:], p1)
         nc.sync.dma_start(p2_sb[:], p2)
-        w2_raw = sb("w2_raw", [P, PACK, H], F32)
-        nc.sync.dma_start(w2_raw[:], w2.rearrange("(p j) c -> p j c", j=PACK))
+        w2_raw = []
+        for h in range(2):
+            raw = sb("w2_raw%d" % h, [P, PACK, H // 2], F32)
+            nc.sync.dma_start(raw[:], w2[:, h * 256 : (h + 1) * 256].rearrange("(p j) c -> p j c", j=PACK))
+            w2_raw.append(raw)
         gn_sb = sb("gn_sb", [P, PACK], F32)
         nc.sync.dma_start(gn_sb[:], gn.rearrange("(p t) o -> p (t o)", t=PACK))
         w3_raw = sb("w3_raw", [P, PACK, N], F32)
@@ -72,19 +75,22 @@ def tile_picked_kerndens_none_p_kernel(
         xa_s = sb("xa_s", [P, S], U8)
         xb_s = sb("xb_s", [P, S], U8)
         xa_w = sb("xa_w", [P, S], U32)
-        xb_w = sb("xb_w", [P, S], U32)
         nc.vector.tensor_copy(xa_s[:], xs_sb[:].indirect(offs_sb[:]))
         nc.vector.tensor_copy(xb_s[:], xs_sb[:].indirect(two_sb[:]))
         nc.vector.tensor_copy(xa_w[:], xw_sb[:].bitcast(U32).indirect(offs_sb[:]))
-        nc.vector.tensor_copy(xb_w[:], xw_sb[:].bitcast(U32).indirect(two_sb[:]))
 
         w1_g = sb("w1_g", [P, PACK * H], BF16)
         w1_gv = w1_g[:].rearrange("p (t m j) -> p m j t", t=PACK, j=PACK)
         nc.scalar.copy(w1_gv[:, 0:64], w1_raw[0][:].rearrange("p j (m t) -> p m j t", t=PACK))
-        nc.vector.tensor_copy(w1_gv[:, 64:128], w1_raw[1][:].rearrange("p j (m t) -> p m j t", t=PACK))
+        late = w1_raw[1][:].rearrange("p j (m t) -> p m j t", t=PACK)
+        nc.vector.tensor_copy(w1_gv[:, 64:108], late[:, 0:44])
+        nc.scalar.copy(w1_gv[:, 108:128], late[:, 44:64])
         w1_c = sb("w1_c", [P, H], U32)
         w1_s = sb("w1_s", [P, H], U8)
-        y_cp = [sb("y_cp%d" % t, [P, S], F32) for t in range(PACK)]
+        y_cp01 = [sb("y_cp%d" % t, [P, S], F32) for t in range(2)]
+        y_cp23 = sb("y_cp23", [P, 2 * S], F32)
+        y_cp = [y_cp01[0][:], y_cp01[1][:], y_cp23[:, :S], y_cp23[:, S:]]
+        y_acc = []
         for t in range(PACK):
             cols = slice(t * P, (t + 1) * P)
             nc.vector.quantize_mx(out=w1_c[:, cols].bitcast(FP8X4), scales=w1_s[:, cols], in_=w1_g[:, t * 512 : (t + 1) * 512])
@@ -93,31 +99,32 @@ def tile_picked_kerndens_none_p_kernel(
                 out=acc[:], lhsT=w1_c[:, cols].bitcast(FP8X4), lhsT_scale=w1_s[:, cols],
                 rhs=xa_w[:].bitcast(FP8X4), rhs_scale=xa_s[:], start=True, stop=True,
             )
-            nc.scalar.copy(y_win[t][:, :S], acc[:])
+            y_acc.append(acc)
+        xb_w = sb("xb_w", [P, S], U32, tag="w1_g")
+        nc.vector.tensor_copy(xb_w[:], xw_sb[:].bitcast(U32).indirect(two_sb[:]))
+
+        def fetch_y(t):
+            nc.scalar.copy(y_win[t][:, :S], y_acc[t][:])
             if t == 0:
-                nc.vector.tensor_copy(y_cp[t][:], y_win[t][:, :S])
+                nc.scalar.copy(y_cp[t], y_acc[t][:])
             else:
-                nc.sync.dma_start(y_cp[t][:], y_win[t][:, :S])
+                nc.sync.dma_start(y_cp[t], y_win[t][:, :S])
+
+        fetch_y(0)
+        fetch_y(1)
 
         w2_g = sb("w2_g", [P, PACK * H], BF16)
-        nc.vector.tensor_copy(
-            w2_g[:].rearrange("p (t m j) -> p m j t", t=PACK, j=PACK), w2_raw[:].rearrange("p j (m t) -> p m j t", t=PACK)
-        )
+        w2_gv = w2_g[:].rearrange("p (t m j) -> p m j t", t=PACK, j=PACK)
+        nc.vector.tensor_copy(w2_gv[:, 0:64], w2_raw[0][:].rearrange("p j (m t) -> p m j t", t=PACK))
+        nc.scalar.copy(w2_gv[:, 64:128], w2_raw[1][:].rearrange("p j (m t) -> p m j t", t=PACK))
+        fetch_y(2)
+        fetch_y(3)
         w2_c = sb("w2_c", [P, H], U32)
         w2_s = sb("w2_s", [P, H], U8)
         nc.vector.quantize_mx(out=w2_c[:].bitcast(FP8X4), scales=w2_s[:], in_=w2_g[:])
 
-        kk = []
         c_win = []
         for t in range(PACK):
-            d = sb("d%d" % t, [P, 2 * S], F32)
-            nc.vector.tensor_tensor(d[:, :S], y_win[t][:].indirect(p1_sb[:]), y_cp[t][:], ALU.subtract)
-            nc.vector.tensor_tensor(d[:, S:], y_win[t][:].indirect(p2_sb[:]), y_cp[t][:], ALU.subtract)
-            sq = sb("sq%d" % t, [P, 2 * S], F32)
-            nc.scalar.activation(sq[:], d[:], ACT.Square)
-            k = sb("k%d" % t, [P, 2 * S], F32)
-            nc.scalar.activation(k[:], sq[:], ACT.Exp, scale=-0.5)
-            kk.append(k)
             cols = slice(t * P, (t + 1) * P)
             acc = bank(4 + t)
             nc.tensor.matmul_mx(
@@ -127,6 +134,31 @@ def tile_picked_kerndens_none_p_kernel(
             cw = sb("c_win%d" % t, [P, S], F32)
             nc.scalar.activation(cw[:], acc[:], ACT.Copy, scale=gn_sb[:, t : t + 1])
             c_win.append(cw)
+
+        w3_g = sb("w3_g", [P, PACK * N], BF16)
+        nc.scalar.copy(
+            w3_g[:].rearrange("p (c i j) -> p c j i", i=4, j=PACK), w3_raw[:].rearrange("p j (c i) -> p c j i", i=4)
+        )
+        w3_c = sb("w3_c", [P, N], U32)
+        w3_s = sb("w3_s", [P, N], U8)
+        nc.vector.quantize_mx(out=w3_c[:].bitcast(FP8X4), scales=w3_s[:], in_=w3_g[:])
+
+        kk = []
+        for t in range(PACK):
+            d = sb("d%d" % t, [P, 2 * S], F32)
+            nc.vector.tensor_tensor(d[:, :S], y_win[t][:].indirect(p1_sb[:]), y_cp[t], ALU.subtract)
+            nc.vector.tensor_tensor(d[:, S:], y_win[t][:].indirect(p2_sb[:]), y_cp[t], ALU.subtract)
+            sq = sb("sq%d" % t, [P, 2 * S], F32)
+            nc.scalar.activation(sq[:], d[:], ACT.Square)
+            k = sb("k%d" % t, [P, 2 * S], F32)
+            nc.scalar.activation(k[:], sq[:], ACT.Exp, scale=-0.5)
+            kk.append(k)
+
+        def dealt(acc):
+            return acc[:].rearrange("j (u e p) -> j u p e", u=2, e=2)
+
+        def plain(tile):
+            return tile[:].rearrange("j (u p e) -> j u p e", u=2, e=2)
 
         den = [bank(b) for b in range(4)]
         for t in range(PACK):
@@ -138,66 +170,67 @@ def tile_picked_kerndens_none_p_kernel(
                     )
         rr = []
         for b in range(4):
-            dsq = sb("dsq%d" % b, [P, H], F32)
-            nc.scalar.activation(
-                dsq[:].rearrange("j (p t) -> j p t", t=PACK), den[b][:].rearrange("j (t p) -> j p t", t=PACK), ACT.Square, bias=0.5
-            )
+            rs = sb("rs%d" % b, [P, H], F32)
+            nc.scalar.activation(plain(rs), dealt(den[b]), ACT.Abs_reciprocal_sqrt, bias=0.5)
             r = sb("r%d" % b, [P, H], F32)
-            nc.scalar.activation(r[:], dsq[:], ACT.Abs_reciprocal_sqrt)
+            nc.scalar.activation(r[:], rs[:], ACT.Square)
             rr.append(r)
 
-        w3_g = sb("w3_g", [P, PACK * N], BF16)
-        nc.scalar.copy(
-            w3_g[:].rearrange("p (c i j) -> p c j i", i=4, j=PACK), w3_raw[:].rearrange("p j (c i) -> p c j i", i=4)
-        )
-        w3_c = sb("w3_c", [P, N], U32)
-        w3_s = sb("w3_s", [P, N], U8)
-        nc.vector.quantize_mx(out=w3_c[:].bitcast(FP8X4), scales=w3_s[:], in_=w3_g[:])
+        num = [bank(4 + b) for b in range(4)]
 
-        for h in range(2):
-            js = slice(h * HALF, (h + 1) * HALF)
-            ls = slice(h * HALF // 16, (h + 1) * HALF // 16)
-            num = [bank(4 + 2 * h + b) for b in range(2)]
-            for t in range(PACK):
-                n = sb("n%d_%d" % (h, t), [P, 2 * HALF], F32)
-                nc.vector.tensor_tensor(n[:, :HALF], c_win[t][:].indirect(p1_sb[:, ls]), kk[t][:, h * HALF : (h + 1) * HALF], ALU.mult)
-                nc.vector.tensor_tensor(n[:, HALF:], c_win[t][:].indirect(p2_sb[:, ls]), kk[t][:, S + h * HALF : S + (h + 1) * HALF], ALU.mult)
-                for b in range(2):
-                    for s in range(2):
-                        nc.tensor.matmul(
-                            num[b][:, t * P : (t + 1) * P], lhsT=n[:, s * HALF + b * P : s * HALF + (b + 1) * P], rhs=ident[:],
-                            is_transpose=True, start=(s == 0), stop=(s == 1),
-                        )
-            zw = bank(h)
-            for b in range(2):
-                zt = sb("zt%d_%d" % (h, b), [P, H], BF16)
-                nc.vector.tensor_tensor(
-                    zt[:].rearrange("j (p t) -> j p t", t=PACK), num[b][:].rearrange("j (t p) -> j p t", t=PACK),
-                    rr[2 * h + b][:].rearrange("j (p t) -> j p t", t=PACK), ALU.mult,
-                )
-                words = zt[:].bitcast(F32)
-                for u in range(2):
-                    nc.tensor.transpose(zw[:, (2 * b + u) * P : (2 * b + u + 1) * P], words[:, u : H // 2 : 2], ident[:])
-            z_g = sb("z_g%d" % h, [P, PACK * HALF], BF16)
+        def numerators(t, b0, nb, tag):
+            w = nb * P
+            ls = slice(b0 * P // 16, (b0 * P + w) // 16)
+            n = sb("n%d_%d" % (t, b0), [P, 2 * w], F32, tag=tag)
+            nc.vector.tensor_tensor(n[:, :w], c_win[t][:].indirect(p1_sb[:, ls]), kk[t][:, b0 * P : b0 * P + w], ALU.mult)
+            nc.vector.tensor_tensor(n[:, w:], c_win[t][:].indirect(p2_sb[:, ls]), kk[t][:, S + b0 * P : S + b0 * P + w], ALU.mult)
+            for b in range(nb):
+                for s in range(2):
+                    nc.tensor.matmul(
+                        num[b0 + b][:, t * P : (t + 1) * P], lhsT=n[:, s * w + b * P : s * w + (b + 1) * P], rhs=ident[:],
+                        is_transpose=True, start=(s == 0), stop=(s == 1),
+                    )
+
+        def finish(b):
+            zt = sb("zt%d" % b, [P, H], BF16, tag="z_g%d" % (b - 2) if b >= 2 else None)
+            nc.vector.tensor_tensor(plain(zt), dealt(num[b]), plain(rr[b]), ALU.mult)
+            words = zt[:].bitcast(F32)
+            zw = bank(b)
+            for u in range(2):
+                nc.tensor.transpose(zw[:, u * P : (u + 1) * P], words[:, u * P : (u + 1) * P], ident[:])
+            z_g = sb("z_g%d" % b, [P, PACK * P], BF16)
             nc.scalar.copy(
-                z_g[:].bitcast(F32).rearrange("p (b j u) -> p b j u", b=2, u=2), zw[:].rearrange("p (b u j) -> p b j u", b=2, u=2)
+                z_g[:].bitcast(F32).rearrange("p (j u) -> p j u", u=2), zw[:, : 2 * P].rearrange("p (u j) -> p j u", u=2)
             )
-            z_c = sb("z_c%d" % h, [P, HALF], U32)
-            z_s = sb("z_s%d" % h, [P, HALF], U8)
+            z_c = sb("z_c%d" % b, [P, P], U32)
+            z_s = sb("z_s%d" % b, [P, P], U8)
             nc.vector.quantize_mx(out=z_c[:].bitcast(FP8X4), scales=z_s[:], in_=z_g[:])
-            for g in range(2):
-                acc = bank(2 + 2 * h + g)
-                for a in range(2):
-                    cols = slice((2 * g + a) * P, (2 * g + a + 1) * P)
+            if b < 3:
+                parts = [(4 + b, 0, 4, nc.vector.tensor_copy if b == 1 else nc.scalar.copy)]
+            else:
+                parts = [(4 + b, 0, 2, nc.vector.tensor_copy), (0, 2, 2, nc.scalar.copy)]
+            for where, a0, na, fetch in parts:
+                acc = bank(where)
+                for a in range(na):
+                    cols = slice((a0 + a) * P, (a0 + a + 1) * P)
                     nc.tensor.matmul_mx(
-                        out=acc[:, a * HALF : (a + 1) * HALF], lhsT=w3_c[:, cols].bitcast(FP8X4), lhsT_scale=w3_s[:, cols],
+                        out=acc[:, a * P : (a + 1) * P], lhsT=w3_c[:, cols].bitcast(FP8X4), lhsT_scale=w3_s[:, cols],
                         rhs=z_c[:].bitcast(FP8X4), rhs_scale=z_s[:], start=True, stop=True,
                     )
-                res = sb("res%d_%d" % (h, g), [P, 2 * HALF], F32)
-                if g == 0:
-                    nc.scalar.copy(res[:], acc[:])
-                else:
-                    nc.vector.tensor_copy(res[:], acc[:])
+                res = sb("res%d_%d" % (b, a0), [P, na * P], F32)
+                fetch(res[:], acc[:, : na * P])
                 nc.sync.dma_start(
-                    out[g * 256 : (g + 1) * 256, js].rearrange("(a p) j -> p a j", a=2), res[:].rearrange("p (a j) -> p a j", a=2)
+                    out[a0 * P : (a0 + na) * P, b * P : (b + 1) * P].rearrange("(a p) j -> p a j", a=na),
+                    res[:].rearrange("p (a j) -> p a j", a=na),
                 )
+
+        for t in range(PACK):
+            numerators(t, 0, 3, "n_ring%d" % (t % 2))
+        numerators(0, 3, 1, "n_ring0")
+        numerators(1, 3, 1, "n_ring1")
+        finish(0)
+        numerators(2, 3, 1, "r0")
+        finish(1)
+        numerators(3, 3, 1, "r1")
+        finish(2)
+        finish(3)

from contextlib import ExitStack

import concourse.mybir as mybir
from concourse.masks import make_identity

K, T, S, N, H = 512, 2048, 512, 512, 512
FLOPS = 2 * K * H * S * 2 + 2 * H * N * S

F32 = mybir.dt.float32
BF16 = mybir.dt.bfloat16
I32 = mybir.dt.int32
U32 = mybir.dt.uint32
U16 = mybir.dt.uint16
U8 = mybir.dt.uint8
FP8X4 = mybir.dt.float8_e4m3fn_x4
ALU = mybir.AluOpType
ACT = mybir.ActivationFunctionType

P = 128
PACK = 4
HALF = S // 2


def tile_picked_kerndens_none_p_kernel(
    tc, x_words, x_scales, w1, w2, gn, w3, offs, two, p1, p2, out
):
    nc = tc.nc
    with ExitStack() as ctx:
        keep = ctx.enter_context(tc.tile_pool(name="keep", bufs=1))
        psum = ctx.enter_context(tc.psum_pool(name="psum", bufs=1))

        def bank(b):
            return psum.tile([P, 512], F32, name="bank%d" % b)

        def sb(name, shape, dtype, tag=None):
            return keep.tile(shape, dtype, name=name, tag=tag or name, align_bytes=64)

        offs_sb = keep.tile([P, S // 16], U16, name="offs_sb")
        two_sb = keep.tile([P, S // 16], U16, name="two_sb")
        p1_sb = keep.tile([P, S // 16], U16, name="p1_sb")
        p2_sb = keep.tile([P, S // 16], U16, name="p2_sb")
        xs_sb = sb("xs_sb", [P, T], U8)
        xw_sb = sb("xw_sb", [P, T], I32)
        nc.sync.dma_start(offs_sb[:], offs)
        nc.sync.dma_start(two_sb[:], two)
        for q in range(4):
            rows = x_scales[0, 4 * q : 4 * q + 4, :].bitcast(I32)
            nc.sync.dma_start(
                xs_sb[32 * q : 32 * q + 32, :].bitcast(I32), rows.unsqueeze(0).broadcast_to([8, 4, T // 4])
            )
        nc.sync.dma_start(xw_sb[:], x_words[0].rearrange("p n t -> p (n t)").bitcast(I32))
        w1_raw = []
        for h in range(2):
            raw = sb("w1_raw%d" % h, [P, PACK, H // 2], F32)
            nc.sync.dma_start(raw[:], w1[:, h * 256 : (h + 1) * 256].rearrange("(p j) c -> p j c", j=PACK))
            w1_raw.append(raw)
        nc.sync.dma_start(p1_sb[:], p1)
        nc.sync.dma_start(p2_sb[:], p2)
        w2_raw = []
        for h in range(2):
            raw = sb("w2_raw%d" % h, [P, PACK, H // 2], F32)
            nc.sync.dma_start(raw[:], w2[:, h * 256 : (h + 1) * 256].rearrange("(p j) c -> p j c", j=PACK))
            w2_raw.append(raw)
        gn_sb = sb("gn_sb", [P, PACK], F32)
        nc.sync.dma_start(gn_sb[:], gn.rearrange("(p t) o -> p (t o)", t=PACK))
        w3_raw = sb("w3_raw", [P, PACK, N], F32)
        nc.sync.dma_start(w3_raw[:], w3.rearrange("(p j) c -> p j c", j=PACK))

        ident = sb("ident", [P, P], F32)
        make_identity(nc, ident[:])
        y_win = [sb("y_win%d" % t, [P, 2 * S], F32) for t in range(PACK)]
        for t in range(PACK):
            nc.gpsimd.memset(y_win[t][:, S:], 0.0)

        xa_s = sb("xa_s", [P, S], U8)
        xb_s = sb("xb_s", [P, S], U8)
        xa_w = sb("xa_w", [P, S], U32)
        nc.vector.tensor_copy(xa_s[:], xs_sb[:].indirect(offs_sb[:]))
        nc.vector.tensor_copy(xb_s[:], xs_sb[:].indirect(two_sb[:]))
        nc.vector.tensor_copy(xa_w[:], xw_sb[:].bitcast(U32).indirect(offs_sb[:]))

        w1_g = sb("w1_g", [P, PACK * H], BF16)
        w1_gv = w1_g[:].rearrange("p (t m j) -> p m j t", t=PACK, j=PACK)
        nc.scalar.copy(w1_gv[:, 0:64], w1_raw[0][:].rearrange("p j (m t) -> p m j t", t=PACK))
        late = w1_raw[1][:].rearrange("p j (m t) -> p m j t", t=PACK)
        nc.vector.tensor_copy(w1_gv[:, 64:108], late[:, 0:44])
        nc.scalar.copy(w1_gv[:, 108:128], late[:, 44:64])
        w1_c = sb("w1_c", [P, H], U32)
        w1_s = sb("w1_s", [P, H], U8)
        y_cp01 = [sb("y_cp%d" % t, [P, S], F32) for t in range(2)]
        y_cp23 = sb("y_cp23", [P, 2 * S], F32)
        y_cp = [y_cp01[0][:], y_cp01[1][:], y_cp23[:, :S], y_cp23[:, S:]]
        y_acc = []
        for t in range(PACK):
            cols = slice(t * P, (t + 1) * P)
            nc.vector.quantize_mx(out=w1_c[:, cols].bitcast(FP8X4), scales=w1_s[:, cols], in_=w1_g[:, t * 512 : (t + 1) * 512])
            acc = bank(t)
            nc.tensor.matmul_mx(
                out=acc[:], lhsT=w1_c[:, cols].bitcast(FP8X4), lhsT_scale=w1_s[:, cols],
                rhs=xa_w[:].bitcast(FP8X4), rhs_scale=xa_s[:], start=True, stop=True,
            )
            y_acc.append(acc)
        xb_w = sb("xb_w", [P, S], U32, tag="w1_g")
        nc.vector.tensor_copy(xb_w[:], xw_sb[:].bitcast(U32).indirect(two_sb[:]))

        def fetch_y(t):
            nc.scalar.copy(y_win[t][:, :S], y_acc[t][:])
            if t == 0:
                nc.scalar.copy(y_cp[t], y_acc[t][:])
            else:
                nc.sync.dma_start(y_cp[t], y_win[t][:, :S])

        fetch_y(0)
        fetch_y(1)

        w2_g = sb("w2_g", [P, PACK * H], BF16)
        w2_gv = w2_g[:].rearrange("p (t m j) -> p m j t", t=PACK, j=PACK)
        nc.vector.tensor_copy(w2_gv[:, 0:64], w2_raw[0][:].rearrange("p j (m t) -> p m j t", t=PACK))
        nc.scalar.copy(w2_gv[:, 64:128], w2_raw[1][:].rearrange("p j (m t) -> p m j t", t=PACK))
        fetch_y(2)
        fetch_y(3)
        w2_c = sb("w2_c", [P, H], U32)
        w2_s = sb("w2_s", [P, H], U8)
        nc.vector.quantize_mx(out=w2_c[:].bitcast(FP8X4), scales=w2_s[:], in_=w2_g[:])

        c_win = []
        for t in range(PACK):
            cols = slice(t * P, (t + 1) * P)
            acc = bank(4 + t)
            nc.tensor.matmul_mx(
                out=acc[:], lhsT=w2_c[:, cols].bitcast(FP8X4), lhsT_scale=w2_s[:, cols],
                rhs=xb_w[:].bitcast(FP8X4), rhs_scale=xb_s[:], start=True, stop=True,
            )
            cw = sb("c_win%d" % t, [P, S], F32)
            nc.scalar.activation(cw[:], acc[:], ACT.Copy, scale=gn_sb[:, t : t + 1])
            c_win.append(cw)

        w3_g = sb("w3_g", [P, PACK * N], BF16)
        nc.scalar.copy(
            w3_g[:].rearrange("p (c i j) -> p c j i", i=4, j=PACK), w3_raw[:].rearrange("p j (c i) -> p c j i", i=4)
        )
        w3_c = sb("w3_c", [P, N], U32)
        w3_s = sb("w3_s", [P, N], U8)
        nc.vector.quantize_mx(out=w3_c[:].bitcast(FP8X4), scales=w3_s[:], in_=w3_g[:])

        kk = []
        for t in range(PACK):
            d = sb("d%d" % t, [P, 2 * S], F32)
            nc.vector.tensor_tensor(d[:, :S], y_win[t][:].indirect(p1_sb[:]), y_cp[t], ALU.subtract)
            nc.vector.tensor_tensor(d[:, S:], y_win[t][:].indirect(p2_sb[:]), y_cp[t], ALU.subtract)
            sq = sb("sq%d" % t, [P, 2 * S], F32)
            nc.scalar.activation(sq[:], d[:], ACT.Square)
            k = sb("k%d" % t, [P, 2 * S], F32)
            nc.scalar.activation(k[:], sq[:], ACT.Exp, scale=-0.5)
            kk.append(k)

        def dealt(acc):
            return acc[:].rearrange("j (u e p) -> j u p e", u=2, e=2)

        def plain(tile):
            return tile[:].rearrange("j (u p e) -> j u p e", u=2, e=2)

        den = [bank(b) for b in range(4)]
        for t in range(PACK):
            for b in range(4):
                for s in range(2):
                    nc.tensor.matmul(
                        den[b][:, t * P : (t + 1) * P], lhsT=kk[t][:, s * S + b * P : s * S + (b + 1) * P], rhs=ident[:],
                        is_transpose=True, start=(s == 0), stop=(s == 1),
                    )
        rr = []
        for b in range(4):
            rs = sb("rs%d" % b, [P, H], F32)
            nc.scalar.activation(plain(rs), dealt(den[b]), ACT.Abs_reciprocal_sqrt, bias=0.5)
            r = sb("r%d" % b, [P, H], F32)
            nc.scalar.activation(r[:], rs[:], ACT.Square)
            rr.append(r)

        num = [bank(4 + b) for b in range(4)]

        def numerators(t, b0, nb, tag):
            w = nb * P
            ls = slice(b0 * P // 16, (b0 * P + w) // 16)
            n = sb("n%d_%d" % (t, b0), [P, 2 * w], F32, tag=tag)
            nc.vector.tensor_tensor(n[:, :w], c_win[t][:].indirect(p1_sb[:, ls]), kk[t][:, b0 * P : b0 * P + w], ALU.mult)
            nc.vector.tensor_tensor(n[:, w:], c_win[t][:].indirect(p2_sb[:, ls]), kk[t][:, S + b0 * P : S + b0 * P + w], ALU.mult)
            for b in range(nb):
                for s in range(2):
                    nc.tensor.matmul(
                        num[b0 + b][:, t * P : (t + 1) * P], lhsT=n[:, s * w + b * P : s * w + (b + 1) * P], rhs=ident[:],
                        is_transpose=True, start=(s == 0), stop=(s == 1),
                    )

        def finish(b):
            zt = sb("zt%d" % b, [P, H], BF16, tag="z_g%d" % (b - 2) if b >= 2 else None)
            nc.vector.tensor_tensor(plain(zt), dealt(num[b]), plain(rr[b]), ALU.mult)
            words = zt[:].bitcast(F32)
            zw = bank(b)
            for u in range(2):
                nc.tensor.transpose(zw[:, u * P : (u + 1) * P], words[:, u * P : (u + 1) * P], ident[:])
            z_g = sb("z_g%d" % b, [P, PACK * P], BF16)
            nc.scalar.copy(
                z_g[:].bitcast(F32).rearrange("p (j u) -> p j u", u=2), zw[:, : 2 * P].rearrange("p (u j) -> p j u", u=2)
            )
            z_c = sb("z_c%d" % b, [P, P], U32)
            z_s = sb("z_s%d" % b, [P, P], U8)
            nc.vector.quantize_mx(out=z_c[:].bitcast(FP8X4), scales=z_s[:], in_=z_g[:])
            if b < 3:
                parts = [(4 + b, 0, 4, nc.vector.tensor_copy if b == 1 else nc.scalar.copy)]
            else:
                parts = [(4 + b, 0, 2, nc.vector.tensor_copy), (0, 2, 2, nc.scalar.copy)]
            for where, a0, na, fetch in parts:
                acc = bank(where)
                for a in range(na):
                    cols = slice((a0 + a) * P, (a0 + a + 1) * P)
                    nc.tensor.matmul_mx(
                        out=acc[:, a * P : (a + 1) * P], lhsT=w3_c[:, cols].bitcast(FP8X4), lhsT_scale=w3_s[:, cols],
                        rhs=z_c[:].bitcast(FP8X4), rhs_scale=z_s[:], start=True, stop=True,
                    )
                res = sb("res%d_%d" % (b, a0), [P, na * P], F32)
                fetch(res[:], acc[:, : na * P])
                nc.sync.dma_start(
                    out[a0 * P : (a0 + na) * P, b * P : (b + 1) * P].rearrange("(a p) j -> p a j", a=na),
                    res[:].rearrange("p (a j) -> p a j", a=na),
                )

        for t in range(PACK):
            numerators(t, 0, 3, "n_ring%d" % (t % 2))
        numerators(0, 3, 1, "n_ring0")
        numerators(1, 3, 1, "n_ring1")
        finish(0)
        numerators(2, 3, 1, "r0")
        finish(1)
        numerators(3, 3, 1, "r1")
        finish(2)
        finish(3)
